import numpy as np, ml_dtypes
CORES = [0,1]
N = 2
ROOT = 0
def setup_inputs(rng):
    return {"x": rng.standard_normal((N, 128, 4), dtype=np.float32).astype(ml_dtypes.bfloat16)}
def reference(x):
    y = np.full(x.shape, np.nan, x.dtype)
    y[ROOT] = x.sum(axis=0, dtype=np.float64).astype(x.dtype)
    return {"y": y}

from concourse.mybir import AluOpType

SCRATCH = {
    "stage": ("sbuf", [128, 4], "bfloat16"),
    "land": ("sbuf", [128, 4], "bfloat16"),
}
SEMAPHORES = ["loaded", "stored", "arrived", "sent"]

ENGINES = 16


def rank_program(g, core, T, topo):
    rank = T.rank_of(core)
    if rank is None:
        return
    root = T.cores[0]

    if core != root:
        g.dma_start(T.stage[:], T.x[:]).then_inc(T.sem.loaded, 16)
        g.wait_ge(T.sem.loaded, 16)
        rid, pid, sengine = topo.addr(root)
        g.remote_dma(T.land[:], T.stage[:], T.sem.arrived, T.sem.sent, pid, rid, topo.mask(core, root))
        g.wait_ge(T.sem.sent, ENGINES)
        return

    g.dma_start(T.y[:], T.x[:]).then_inc(T.sem.loaded, 16)
    g.wait_ge(T.sem.loaded, 16)
    g.wait_ge(T.sem.arrived, ENGINES)
    g.dma_start(T.y[:], T.land[:], accum_op=AluOpType.add).then_inc(T.sem.stored, 16)
    g.wait_ge(T.sem.stored, 16)
